import numpy as np
import ml_dtypes


def mxq(x, axis, fmt="e4m3"):
    dtype, down = {"e4m3": (ml_dtypes.float8_e4m3fn, 7), "e5m2": (ml_dtypes.float8_e5m2, 14)}[fmt]
    v = np.moveaxis(np.asarray(x, np.float32).astype(ml_dtypes.bfloat16).astype(np.float64), axis, -1)
    blocks = v.reshape(v.shape[:-1] + (-1, 32))
    amax = np.abs(blocks).max(-1, keepdims=True)
    byte = np.maximum(np.where(amax > 0, np.frexp(amax)[1] - 1 + 127, 0) - down, 1)
    scale = np.exp2(byte - 127.0)
    codes = (blocks / scale).astype(np.float32).astype(dtype).astype(np.float64)
    return np.moveaxis((codes * scale).reshape(v.shape), -1, axis)


WIDE = False


def mx_kscale(k):
    if not WIDE:
        return np.ones(k)
    levels = np.array([10, -10, 5, -5, 0])
    if k % 512:
        return np.exp2(np.random.permutation(np.resize(levels, k // 32))).repeat(32)
    a = np.empty((k // 512, 16))
    for p in range(k // 512):
        a[p, :8] = np.random.permutation(np.resize(levels, 8))
        for g in range(8):
            far = levels[np.abs(levels - a[p, g]) >= 10]
            a[p, g + 8] = far[np.random.randint(len(far))]
    return np.exp2(a.ravel()).repeat(32)


def f64(x):
    return np.asarray(x).astype(np.float64)


def striped(idx):
    return np.tile(idx.reshape(-1, 16).T, (8, 1)).astype(np.uint16)


def unstriped(offs):
    return offs[:16].T.reshape(-1).astype(np.int64)


E2M1 = np.array([0.0, 0.5, 1.0, 1.5, 2.0, 3.0, 4.0, 6.0, -0.0, -0.5, -1.0, -1.5, -2.0, -3.0, -4.0, -6.0])


def pack_weight(w, fmt):
    k, n = w.shape
    w = f64(np.asarray(w, np.float32).astype(ml_dtypes.bfloat16)).reshape(k // 32, 32, n)
    amax = np.abs(w).max(1)
    if fmt == "e4m3":
        byte = np.frexp(amax)[1] - 1 + 127 - 7
    else:
        mant, ex = np.frexp(amax / 6.0)
        byte = np.where(mant > 0.5, ex, ex - 1) + 127
    byte = np.clip(np.where(amax > 0, byte, 1), 1, 254)
    scaled = (w * np.exp2(127.0 - byte)[:, None, :]).reshape(k, n).astype(np.float32)
    by_word = np.ascontiguousarray(scaled.reshape(k // 512, 128, 4, n).transpose(0, 1, 3, 2))
    if fmt == "e4m3":
        words = by_word.astype(ml_dtypes.float8_e4m3fn).view(np.uint8)
    else:
        c = by_word.astype(ml_dtypes.float4_e2m1fn).view(np.uint8) & 0xF
        words = (c[..., 0::2] | (c[..., 1::2] << 4)).reshape(k // 512, 128, 2 * n)
    return np.ascontiguousarray(words), np.ascontiguousarray(byte.astype(np.uint8).reshape(k // 512, 16, n))


def unpack_weight(words, scales, fmt):
    g, _, n = scales.shape
    words = np.ascontiguousarray(words).reshape(g, 128, n, -1)
    if fmt == "e4m3":
        vals = words.view(ml_dtypes.float8_e4m3fn).astype(np.float64)
    else:
        nib = np.empty((g, 128, n, 4), np.uint8)
        nib[..., 0::2] = words & 0xF
        nib[..., 1::2] = words >> 4
        vals = E2M1[nib]
    vals = vals * np.repeat(np.exp2(scales.astype(np.float64) - 127.0), 8, axis=1)[..., None]
    return vals.transpose(0, 1, 3, 2).reshape(g * 512, n)


def gelu(v):
    return 0.5 * v * (1.0 + np.tanh(np.sqrt(2.0 / np.pi) * (v + 0.044715 * v**3)))


K, H, N, T, S, P = 1536, 1024, 768, 4096, 1024, 512

def setup_inputs():
    n = np.random.standard_normal
    sk = mx_kscale(K)[:, None]
    u = mx_kscale(H)[:, None]
    tab_words, tab_scales = pack_weight(n((K, T)) * sk, "e4m3")
    w4_words, w4_scales = pack_weight(0.7 * n((K, H)) / np.sqrt(K) / sk, "e2m1")
    w2 = n((H, N)) / np.sqrt(H) / u
    sign = np.random.choice([-1.0, 1.0], H)
    gain = sign * np.random.uniform(0.5, 1.5, H) * u[:, 0]
    perm = np.random.permutation(S)
    return {
        "tab_words": tab_words, "tab_scales": tab_scales,
        "offs": striped(np.random.permutation(T)[:S]),
        "pos1": striped(perm[:P]),
        "pos2": striped(perm[P:]),
        "w4_words": w4_words, "w4_scales": w4_scales,
        "temp": np.random.uniform(0.4, 1.6, H).astype(np.float32),
        "bias": (0.5 * n(H)).astype(np.float32),
        "base": n(H).astype(np.float32),
        "tare": (0.8 * n(H)).astype(np.float32),
        "wgs": np.exp(0.3 * n((128, P))).astype(np.float32),
        "gain": gain.astype(np.float32),
        "w2": w2.astype(np.float32),
        "least": n((N, S)).astype(np.float32),
    }

def reference(tab_words, tab_scales, offs, pos1, pos2, w4_words, w4_scales, temp, bias, base, tare, wgs, gain, w2, least):
    v = unpack_weight(tab_words, tab_scales, "e4m3")[:, unstriped(offs)]
    w4 = unpack_weight(w4_words, w4_scales, "e2m1")
    h = w4.T @ v
    a = np.exp(f64(temp)[:, None] * h[:, unstriped(pos1)] + f64(bias)[:, None])
    a = a - f64(base)[:, None]
    page = h + f64(tare)[:, None]
    page[:, unstriped(pos2)] = np.tile(f64(wgs), (H // 128, 1)) * a
    hq = mxq(f64(gain)[:, None] * page, 0, "e4m3")
    y = mxq(f64(w2), 0, "e4m3").T @ hq
    return np.maximum(y, f64(least))

@@ -1,0 +1,224 @@
+from contextlib import ExitStack
+
+import concourse.mybir as mybir
+
+K, H, N, T, S, NP = 1536, 1024, 768, 4096, 1024, 512
+FLOPS = 2 * K * H * S + 2 * H * N * S
+
+F32 = mybir.dt.float32
+BF16 = mybir.dt.bfloat16
+I32 = mybir.dt.int32
+U32 = mybir.dt.uint32
+U16 = mybir.dt.uint16
+U8 = mybir.dt.uint8
+FP8X4 = mybir.dt.float8_e4m3fn_x4
+FP4X4 = mybir.dt.float4_e2m1fn_x4
+ALU = mybir.AluOpType
+ACT = mybir.ActivationFunctionType
+
+P = 128
+PACK = 4
+BANK = 512
+KP = K // 512
+HP = H // 512
+TILES = H // P
+HALVES = S // BANK
+NT = N // P
+ROW0 = 48
+W2C = 384
+
+
+def tile_list_corner_error_mender_kernel(tc, tab_words, tab_scales, offs, pos1, pos2, w4_words, w4_scales,
+                                                   temp, bias, base, tare, wgs, gain, w2, least, out):
+    nc = tc.nc
+    with ExitStack() as ctx:
+        keep = ctx.enter_context(tc.tile_pool(name="keep", bufs=1))
+        ring = ctx.enter_context(tc.tile_pool(name="ring", bufs=2))
+        psum = ctx.enter_context(tc.psum_pool(name="psum", bufs=8))
+
+        offs_t = keep.tile([P, S // 16], U16, name="offs_t")
+        pos1_t = keep.tile([P, NP // 16], U16, name="pos1_t")
+        pos2_t = keep.tile([P, NP // 16], U16, name="pos2_t")
+        tab_rows = keep.tile([P, T], U8, name="tab_rows", align_bytes=64)
+        w4_rows = keep.tile([P, H], U8, name="w4_rows", align_bytes=64)
+        tab = [keep.tile([P, T], U32, name="tab%d" % a, align_bytes=64) for a in range(KP)]
+        w4_raw = keep.tile([P, KP, 2 * H], U8, name="w4_raw", align_bytes=64)
+
+        tab_flat = tab_scales.rearrange("a q t -> (a q) t").bitcast(I32)
+        nc.sync.dma_start(out=tab_rows[ROW0 + 16 : ROW0 + 48, :].bitcast(I32), in_=tab_flat[16:48, :])
+        nc.sync.dma_start(out=tab_rows[ROW0 : ROW0 + 16, :].bitcast(I32), in_=tab_flat[0:16, :])
+        nc.sync.dma_start(out=offs_t[:], in_=offs)
+        w4_flat = w4_scales.rearrange("a q c -> (a q) c").bitcast(I32)
+        nc.sync.dma_start(out=w4_rows[ROW0 + 16 : ROW0 + 48, :].bitcast(I32), in_=w4_flat[16:48, :])
+        nc.sync.dma_start(out=w4_rows[ROW0 : ROW0 + 16, :].bitcast(I32), in_=w4_flat[0:16, :])
+
+        def load_tab(a):
+            nc.sync.dma_start(out=tab[a][:].bitcast(I32), in_=tab_words[a].rearrange("p t i -> p (t i)").bitcast(I32))
+
+        load_tab(0)
+        nc.sync.dma_start(out=w4_raw[:].bitcast(I32), in_=w4_words.rearrange("a p c -> p a c").bitcast(I32))
+        load_tab(1)
+        load_tab(2)
+        nc.sync.dma_start(out=pos1_t[:], in_=pos1)
+
+        vec = {}
+        for nm, src in (("temp", temp), ("bias", bias), ("tare", tare), ("base", base), ("gain", gain)):
+            vec[nm] = keep.tile([P, HP, PACK], F32, name="v_" + nm)
+            nc.gpsimd.dma_start(out=vec[nm][:], in_=src.rearrange("(b p t) -> p b t", b=HP, t=PACK))
+
+        def col(tile, i):
+            return tile[:, i // PACK, i % PACK : i % PACK + 1]
+
+        wg = keep.tile([P, PACK, NP], F32, name="wg")
+        for q in range(4):
+            nc.sync.dma_start(out=wg[32 * q : 32 * q + 32, :, :], in_=wgs.rearrange("(p t) m -> p t m", t=PACK))
+        nc.sync.dma_start(out=pos2_t[:], in_=pos2)
+        res = [keep.tile([P, S], F32, name="res%d" % n) for n in range(NT)]
+        for n in range(NT):
+            nc.sync.dma_start(out=res[n][:], in_=least[P * n : P * (n + 1), :])
+        w2_raw = [keep.tile([P, PACK, N], F32, name="w2_raw%d" % b) for b in range(HP)]
+        for b in range(HP):
+            nc.sync.dma_start(out=w2_raw[b][:], in_=w2[512 * b : 512 * (b + 1), :].rearrange("(p t) n -> p t n", t=PACK))
+
+        planes = [keep.tile([P, S + H], U8, name="plane%d" % a, align_bytes=64) for a in range(KP)]
+        for t_ in (tab_rows, w4_rows):
+            nc.vector.memset(t_[0:ROW0, :].bitcast(I32), 0)
+            nc.vector.memset(t_[ROW0 + 16 * KP : P, :].bitcast(I32), 0)
+        for a in range(KP):
+            nc.vector.memset(planes[a][:].bitcast(I32), 0)
+
+        picked_rows = keep.tile([P, S], U8, name="picked_rows", align_bytes=64)
+        both_rows = keep.tile([P, S + H], U8, name="both_rows", align_bytes=64)
+        nc.vector.tensor_copy(out=picked_rows[:], in_=tab_rows[:].indirect(offs_t[:]))
+        nc.vector.tensor_copy(out=both_rows[:, S : S + H].rearrange("p (b t m) -> p b t m", b=HP, t=PACK),
+                              in_=w4_rows[:].rearrange("p (b m t) -> p b t m", b=HP, t=PACK))
+        nc.vector.tensor_copy(out=both_rows[:, 0:S].bitcast(I32), in_=picked_rows[:].bitcast(I32))
+        for a in range(KP):
+            for q in range(4):
+                r0 = ROW0 + 16 * a + 4 * q
+                nc.gpsimd.dma_start(out=planes[a][32 * q : 32 * q + 4, :].bitcast(I32), in_=both_rows[r0 : r0 + 4, :].bitcast(I32))
+
+        neg_base = keep.tile([P, HP, PACK], F32, name="neg_base")
+        nc.vector.tensor_scalar(out=neg_base[:], in0=vec["base"][:], scalar1=-1.0, scalar2=None, op0=ALU.mult)
+
+        w4 = [keep.tile([P, 2 * H], U8, name="w4_%d" % a, align_bytes=64) for a in range(KP)]
+        for a in range(KP):
+            nc.scalar.copy(out=w4[a][:].bitcast(U16).rearrange("p (b t m) -> p b t m", b=HP, t=PACK),
+                           in_=w4_raw[:, a, :].bitcast(U16).rearrange("p (b m t) -> p b t m", b=HP, t=PACK))
+
+        picked = [keep.tile([P, S], U32, name="picked%d" % a, align_bytes=64) for a in range(KP)]
+        for a in range(KP - 1):
+            nc.vector.tensor_copy(out=picked[a][:], in_=tab[a][:].indirect(offs_t[:]))
+        for h in range(HALVES):
+            nc.vector.tensor_copy(out=picked[KP - 1][:, BANK * h : BANK * (h + 1)],
+                                  in_=tab[KP - 1][:].indirect(offs_t[:, 32 * h : 32 * (h + 1)]))
+
+        def first_pass(bank, i, h, a):
+            nc.tensor.matmul_mx(
+                out=bank[:],
+                lhsT=w4[a][:, 2 * P * i : 2 * P * (i + 1)].bitcast(FP4X4),
+                lhsT_scale=planes[a][:, S + P * i : S + P * (i + 1)],
+                rhs=picked[a][:, BANK * h : BANK * (h + 1)].bitcast(FP8X4),
+                rhs_scale=planes[a][:, BANK * h : BANK * (h + 1)],
+                start=(a == 0), stop=(a == KP - 1))
+
+        hb = {}
+        EARLY = 4
+        for i in range(EARLY):
+            for h in range(HALVES):
+                hb[i, h] = psum.tile([P, BANK], F32, name="bank")
+        for a in range(KP):
+            for i in range(EARLY):
+                for h in range(HALVES):
+                    first_pass(hb[i, h], i, h, a)
+
+        h_t, page, look, diff = {}, {}, {}, {}
+        gained = [ring.tile([P, PACK, S], BF16, name="gained") for b in range(HP)]
+        a_codes = [keep.tile([P, S], U32, name="a_codes%d" % b, align_bytes=64) for b in range(HP)]
+        a_scales = [keep.tile([P, S], U8, name="a_scales%d" % b, align_bytes=64) for b in range(HP)]
+        w_codes = [keep.tile([P, N], U32, name="w_codes%d" % b, align_bytes=64) for b in range(HP)]
+        w_scales = [keep.tile([P, N], U8, name="w_scales%d" % b, align_bytes=64) for b in range(HP)]
+
+        def leave_psum(i):
+            if i >= EARLY:
+                for h in range(HALVES):
+                    hb[i, h] = psum.tile([P, BANK], F32, name="bank")
+                    for a in range(KP):
+                        first_pass(hb[i, h], i, h, a)
+            h_t[i] = ring.tile([P, S], F32, name="h_t", bufs=3)
+            for h in range(HALVES):
+                nc.scalar.copy(out=h_t[i][:, BANK * h : BANK * (h + 1)], in_=hb[i, h][:])
+            page[i] = ring.tile([P, S], F32, name="page", bufs=4)
+            nc.vector.tensor_scalar(out=page[i][:], in0=h_t[i][:], scalar1=col(vec["tare"], i), scalar2=None, op0=ALU.add)
+
+        def take_look(i):
+            look[i] = ring.tile([P, NP], F32, name="look")
+            nc.scalar.activation(out=look[i][:], in_=h_t[i][:].indirect(pos1_t[:]), func=ACT.Exp,
+                                 bias=col(vec["bias"], i), scale=col(vec["temp"], i))
+
+        def rewrite(i):
+            diff[i] = ring.tile([P, NP], F32, name="diff", bufs=3)
+            nc.scalar.activation(out=diff[i][:], in_=look[i][:], func=ACT.Identity, bias=col(neg_base, i))
+            nc.vector.tensor_tensor(out=page[i][:].indirect(pos2_t[:]), in0=diff[i][:], in1=wg[:, i % PACK, :], op=ALU.mult)
+
+        def weave(dst, src):
+            return (dst.rearrange("p (c i) t -> p c t i", i=4), src.rearrange("p t (c i) -> p c t i", i=4))
+
+        def apply_gain(i):
+            b = i // PACK
+            nc.scalar.activation(out=gained[b][:, i % PACK, :], in_=page[i][:], func=ACT.Copy, scale=col(vec["gain"], i))
+            if i % PACK == PACK - 1:
+                for h in range(HALVES):
+                    cols = slice(BANK * h, BANK * (h + 1))
+                    woven = ring.tile([P, BANK, PACK], BF16, name="woven", align_bytes=64)
+                    o, s = weave(woven[:], gained[b][:, :, cols])
+                    nc.vector.tensor_copy(out=o, in_=s)
+                    nc.vector.quantize_mx(out=a_codes[b][:, cols].bitcast(FP8X4), scales=a_scales[b][:, cols],
+                                          in_=woven[:].rearrange("p c t -> p (c t)"))
+
+        def quantise_w2(j):
+            b, c = divmod(j, N // W2C)
+            cols = slice(W2C * c, W2C * (c + 1))
+            w_woven = ring.tile([P, W2C, PACK], BF16, name="w_woven", align_bytes=64)
+            o, s = weave(w_woven[:], w2_raw[b][:, :, cols])
+            nc.scalar.copy(out=o, in_=s)
+            nc.vector.quantize_mx(out=w_codes[b][:, cols].bitcast(FP8X4), scales=w_scales[b][:, cols],
+                                  in_=w_woven[:].rearrange("p c t -> p (c t)"))
+
+        def second_pass(bank, n, h, b):
+            nc.tensor.matmul_mx(
+                out=bank[:],
+                lhsT=w_codes[b][:, P * n : P * (n + 1)].bitcast(FP8X4),
+                lhsT_scale=w_scales[b][:, P * n : P * (n + 1)],
+                rhs=a_codes[b][:, BANK * h : BANK * (h + 1)].bitcast(FP8X4),
+                rhs_scale=a_scales[b][:, BANK * h : BANK * (h + 1)],
+                start=(b == 0), stop=(b == HP - 1))
+
+        leave_psum(0)
+        for i in range(TILES):
+            if i > 0 and i + 1 < TILES:
+                leave_psum(i + 1)
+            take_look(i)
+            if i >= 2:
+                apply_gain(i - 2)
+            rewrite(i)
+            if i == 0:
+                leave_psum(1)
+            if i >= TILES - 4:
+                quantise_w2(i - (TILES - 4))
+        groups = [(n, h) for h in range(HALVES) for n in range(NT)]
+        yb = {}
+        for g in groups[:8]:
+            yb[g] = psum.tile([P, BANK], F32, name="bank")
+            second_pass(yb[g], g[0], g[1], 0)
+        apply_gain(TILES - 2)
+        apply_gain(TILES - 1)
+        for k, g in enumerate(groups):
+            n, h = g
+            if k >= 8:
+                yb[g] = psum.tile([P, BANK], F32, name="bank")
+                second_pass(yb[g], n, h, 0)
+            second_pass(yb[g], n, h, 1)
+            cols = slice(BANK * h, BANK * (h + 1))
+            nc.vector.tensor_tensor(out=res[n][:, cols], in0=yb[g][:], in1=res[n][:, cols], op=ALU.max)
+            nc.sync.dma_start(out=out[P * n : P * (n + 1), cols], in_=res[n][:, cols])

@@ -64,7 +64,7 @@ def tile_list_corner_error_mender_kernel(tc, tab_words, tab_scales, offs, pos1, 
         vec = {}
         for nm, src in (("temp", temp), ("bias", bias), ("tare", tare), ("base", base), ("gain", gain)):
             vec[nm] = keep.tile([P, HP, PACK], F32, name="v_" + nm)
-            nc.gpsimd.dma_start(out=vec[nm][:], in_=src.rearrange("(b p t) -> p b t", b=HP, t=PACK))
+            (nc.sync if nm == "base" else nc.gpsimd).dma_start(out=vec[nm][:], in_=src.rearrange("(b p t) -> p b t", b=HP, t=PACK))
 
         def col(tile, i):
             return tile[:, i // PACK, i % PACK : i % PACK + 1]
@@ -73,12 +73,12 @@ def tile_list_corner_error_mender_kernel(tc, tab_words, tab_scales, offs, pos1, 
         for q in range(4):
             nc.sync.dma_start(out=wg[32 * q : 32 * q + 32, :, :], in_=wgs.rearrange("(p t) m -> p t m", t=PACK))
         nc.sync.dma_start(out=pos2_t[:], in_=pos2)
-        res = [keep.tile([P, S], F32, name="res%d" % n) for n in range(NT)]
-        for n in range(NT):
-            nc.sync.dma_start(out=res[n][:], in_=least[P * n : P * (n + 1), :])
         w2_raw = [keep.tile([P, PACK, N], F32, name="w2_raw%d" % b) for b in range(HP)]
         for b in range(HP):
             nc.sync.dma_start(out=w2_raw[b][:], in_=w2[512 * b : 512 * (b + 1), :].rearrange("(p t) n -> p t n", t=PACK))
+        res = [keep.tile([P, S], F32, name="res%d" % n) for n in range(NT)]
+        for n in range(NT):
+            nc.sync.dma_start(out=res[n][:], in_=least[P * n : P * (n + 1), :])
 
         planes = [keep.tile([P, S + H], U8, name="plane%d" % a, align_bytes=64) for a in range(KP)]
         for t_ in (tab_rows, w4_rows):
@@ -98,9 +98,6 @@ def tile_list_corner_error_mender_kernel(tc, tab_words, tab_scales, offs, pos1, 
                 r0 = ROW0 + 16 * a + 4 * q
                 nc.gpsimd.dma_start(out=planes[a][32 * q : 32 * q + 4, :].bitcast(I32), in_=both_rows[r0 : r0 + 4, :].bitcast(I32))
 
-        neg_base = keep.tile([P, HP, PACK], F32, name="neg_base")
-        nc.vector.tensor_scalar(out=neg_base[:], in0=vec["base"][:], scalar1=-1.0, scalar2=None, op0=ALU.mult)
-
         w4 = [keep.tile([P, 2 * H], U8, name="w4_%d" % a, align_bytes=64) for a in range(KP)]
         for a in range(KP):
             nc.scalar.copy(out=w4[a][:].bitcast(U16).rearrange("p (b t m) -> p b t m", b=HP, t=PACK),
@@ -112,6 +109,9 @@ def tile_list_corner_error_mender_kernel(tc, tab_words, tab_scales, offs, pos1, 
         for h in range(HALVES):
             nc.vector.tensor_copy(out=picked[KP - 1][:, BANK * h : BANK * (h + 1)],
                                   in_=tab[KP - 1][:].indirect(offs_t[:, 32 * h : 32 * (h + 1)]))
+
+        neg_base = keep.tile([P, HP, PACK], F32, name="neg_base")
+        nc.vector.tensor_scalar(out=neg_base[:], in0=vec["base"][:], scalar1=-1.0, scalar2=None, op0=ALU.mult)
 
         def first_pass(bank, i, h, a):
             nc.tensor.matmul_mx(
@@ -133,7 +133,9 @@ def tile_list_corner_error_mender_kernel(tc, tab_words, tab_scales, offs, pos1, 
                     first_pass(hb[i, h], i, h, a)
 
         h_t, page, look, diff = {}, {}, {}, {}
-        gained = [ring.tile([P, PACK, S], BF16, name="gained") for b in range(HP)]
+        stage = [keep.tile([P, 2 * W2C], F32, name="stage%d" % k, align_bytes=64) for k in range(3)]
+        gained = keep.tile([P, PACK, S], BF16, name="gained")
+        paired = keep.tile([P, 2, S, 2], BF16, name="paired")
         a_codes = [keep.tile([P, S], U32, name="a_codes%d" % b, align_bytes=64) for b in range(HP)]
         a_scales = [keep.tile([P, S], U8, name="a_scales%d" % b, align_bytes=64) for b in range(HP)]
         w_codes = [keep.tile([P, N], U32, name="w_codes%d" % b, align_bytes=64) for b in range(HP)]
@@ -147,43 +149,64 @@ def tile_list_corner_error_mender_kernel(tc, tab_words, tab_scales, offs, pos1, 
                         first_pass(hb[i, h], i, h, a)
             h_t[i] = ring.tile([P, S], F32, name="h_t", bufs=3)
             for h in range(HALVES):
-                nc.scalar.copy(out=h_t[i][:, BANK * h : BANK * (h + 1)], in_=hb[i, h][:])
+                nc.scalar.activation(out=h_t[i][:, BANK * h : BANK * (h + 1)], in_=hb[i, h][:], func=ACT.Copy)
             page[i] = ring.tile([P, S], F32, name="page", bufs=4)
             nc.vector.tensor_scalar(out=page[i][:], in0=h_t[i][:], scalar1=col(vec["tare"], i), scalar2=None, op0=ALU.add)
 
         def take_look(i):
-            look[i] = ring.tile([P, NP], F32, name="look")
-            nc.scalar.activation(out=look[i][:], in_=h_t[i][:].indirect(pos1_t[:]), func=ACT.Exp,
+            look[i] = stage[i % 3][:, 0:NP]
+            nc.scalar.activation(out=look[i], in_=h_t[i][:].indirect(pos1_t[:]), func=ACT.Exp,
                                  bias=col(vec["bias"], i), scale=col(vec["temp"], i))
 
         def rewrite(i):
             diff[i] = ring.tile([P, NP], F32, name="diff", bufs=3)
-            nc.scalar.activation(out=diff[i][:], in_=look[i][:], func=ACT.Identity, bias=col(neg_base, i))
+            if i == 0:
+                nc.vector.tensor_scalar(out=diff[i][:], in0=look[i], scalar1=col(vec["base"], i), scalar2=None, op0=ALU.subtract)
+            else:
+                nc.scalar.activation(out=diff[i][:], in_=look[i], func=ACT.Identity, bias=col(neg_base, i))
             nc.vector.tensor_tensor(out=page[i][:].indirect(pos2_t[:]), in0=diff[i][:], in1=wg[:, i % PACK, :], op=ALU.mult)
 
         def weave(dst, src):
             return (dst.rearrange("p (c i) t -> p c t i", i=4), src.rearrange("p t (c i) -> p c t i", i=4))
 
+        def quantise_page(b, cols, woven):
+            nc.vector.quantize_mx(out=a_codes[b][:, cols].bitcast(FP8X4), scales=a_scales[b][:, cols],
+                                  in_=woven[:].rearrange("p c t -> p (c t)"))
+
         def apply_gain(i):
-            b = i // PACK
-            nc.scalar.activation(out=gained[b][:, i % PACK, :], in_=page[i][:], func=ACT.Copy, scale=col(vec["gain"], i))
-            if i % PACK == PACK - 1:
+            b, t = divmod(i, PACK)
+            if b == 0:
+                nc.scalar.activation(out=gained[:, t, :], in_=page[i][:], func=ACT.Copy, scale=col(vec["gain"], i))
+            elif t < PACK - 1:
+                nc.scalar.activation(out=paired[:, t // 2, :, t % 2], in_=page[i][:], func=ACT.Copy, scale=col(vec["gain"], i))
+            if t == PACK - 1:
                 for h in range(HALVES):
                     cols = slice(BANK * h, BANK * (h + 1))
                     woven = ring.tile([P, BANK, PACK], BF16, name="woven", align_bytes=64)
-                    o, s = weave(woven[:], gained[b][:, :, cols])
-                    nc.vector.tensor_copy(out=o, in_=s)
-                    nc.vector.quantize_mx(out=a_codes[b][:, cols].bitcast(FP8X4), scales=a_scales[b][:, cols],
-                                          in_=woven[:].rearrange("p c t -> p (c t)"))
+                    if b == 0:
+                        o, s = weave(woven[:], gained[:, :, cols])
+                        nc.vector.tensor_copy(out=o, in_=s)
+                    else:
+                        nc.scalar.activation(out=paired[:, t // 2, cols, t % 2], in_=page[i][:, cols], func=ACT.Copy,
+                                             scale=col(vec["gain"], i))
+                        dt = I32 if h == 0 else U32
+                        o = woven[:].rearrange("p c t -> p (c t)").bitcast(dt).rearrange("p (c u) -> p c u", u=2)
+                        s = paired[:].rearrange("p u c e -> p u (c e)").bitcast(dt)[:, :, cols]
+                        o, s = weave(o, s)
+                        if h == 0:
+                            nc.vector.tensor_copy(out=o, in_=s)
+                        else:
+                            nc.scalar.copy(out=o, in_=s)
+                    quantise_page(b, cols, woven)
 
-        def quantise_w2(j):
+        def quantise_w2(j, spare):
             b, c = divmod(j, N // W2C)
             cols = slice(W2C * c, W2C * (c + 1))
-            w_woven = ring.tile([P, W2C, PACK], BF16, name="w_woven", align_bytes=64)
-            o, s = weave(w_woven[:], w2_raw[b][:, :, cols])
+            w_woven = spare[:].bitcast(BF16)
+            o, s = weave(w_woven.rearrange("p (c t) -> p c t", t=PACK), w2_raw[b][:, :, cols])
             nc.scalar.copy(out=o, in_=s)
             nc.vector.quantize_mx(out=w_codes[b][:, cols].bitcast(FP8X4), scales=w_scales[b][:, cols],
-                                  in_=w_woven[:].rearrange("p c t -> p (c t)"))
+                                  in_=w_woven)
 
         def second_pass(bank, n, h, b):
             nc.tensor.matmul_mx(
@@ -199,13 +222,16 @@ def tile_list_corner_error_mender_kernel(tc, tab_words, tab_scales, offs, pos1, 
             if i > 0 and i + 1 < TILES:
                 leave_psum(i + 1)
             take_look(i)
-            if i >= 2:
+            if 2 <= i < TILES - 1:
                 apply_gain(i - 2)
             rewrite(i)
             if i == 0:
                 leave_psum(1)
-            if i >= TILES - 4:
-                quantise_w2(i - (TILES - 4))
+            if 3 <= i < 5:
+                quantise_w2(i - 3, stage[(i - 1) % 3])
+        apply_gain(TILES - 3)
+        quantise_w2(2, stage[(TILES - 2) % 3])
+        quantise_w2(3, stage[(TILES - 1) % 3])
         groups = [(n, h) for h in range(HALVES) for n in range(NT)]
         yb = {}
         for g in groups[:8]:

@@ -24,8 +24,10 @@ HP = H // 512
 TILES = H // P
 HALVES = S // BANK
 NT = N // P
-ROW0 = 48
+LIVE = 112
 W2C = 384
+CHUNKS = [5]
+ORDER = [0, 4, 1, 2, 3, 5, 6, 7]
 
 
 def tile_list_corner_error_mender_kernel(tc, tab_words, tab_scales, offs, pos1, pos2, w4_words, w4_scales,
@@ -40,78 +42,81 @@ def tile_list_corner_error_mender_kernel(tc, tab_words, tab_scales, offs, pos1, 
         pos1_t = keep.tile([P, NP // 16], U16, name="pos1_t")
         pos2_t = keep.tile([P, NP // 16], U16, name="pos2_t")
         tab_rows = keep.tile([P, T], U8, name="tab_rows", align_bytes=64)
-        w4_rows = keep.tile([P, H], U8, name="w4_rows", align_bytes=64)
-        tab = [keep.tile([P, T], U32, name="tab%d" % a, align_bytes=64) for a in range(KP)]
+        w4_rows = keep.tile([P, H], U8, name="w4_rows", tag="pick1", align_bytes=64)
+        tab = [keep.tile([P, T], U32, name="tab%d" % a, tag="big%d" % a, align_bytes=64) for a in range(KP)]
         w4_raw = keep.tile([P, KP, 2 * H], U8, name="w4_raw", align_bytes=64)
-
-        tab_flat = tab_scales.rearrange("a q t -> (a q) t").bitcast(I32)
-        nc.sync.dma_start(out=tab_rows[ROW0 + 16 : ROW0 + 48, :].bitcast(I32), in_=tab_flat[16:48, :])
-        nc.sync.dma_start(out=tab_rows[ROW0 : ROW0 + 16, :].bitcast(I32), in_=tab_flat[0:16, :])
-        nc.sync.dma_start(out=offs_t[:], in_=offs)
-        w4_flat = w4_scales.rearrange("a q c -> (a q) c").bitcast(I32)
-        nc.sync.dma_start(out=w4_rows[ROW0 + 16 : ROW0 + 48, :].bitcast(I32), in_=w4_flat[16:48, :])
-        nc.sync.dma_start(out=w4_rows[ROW0 : ROW0 + 16, :].bitcast(I32), in_=w4_flat[0:16, :])
 
         def load_tab(a):
             nc.sync.dma_start(out=tab[a][:].bitcast(I32), in_=tab_words[a].rearrange("p t i -> p (t i)").bitcast(I32))
 
+        vec = {}
+
+        def load_vec(nm, src):
+            vec[nm] = keep.tile([P, HP, PACK], F32, name="v_" + nm)
+            nc.sync.dma_start(out=vec[nm][:], in_=src.rearrange("(b p t) -> p b t", b=HP, t=PACK))
+
+        nc.sync.dma_start(out=offs_t[:], in_=offs)
+        nc.sync.dma_start(out=pos1_t[:], in_=pos1)
         load_tab(0)
+        nc.sync.dma_start(out=pos2_t[:], in_=pos2)
+        for nm, src in (("base", base), ("temp", temp), ("bias", bias), ("tare", tare)):
+            load_vec(nm, src)
         nc.sync.dma_start(out=w4_raw[:].bitcast(I32), in_=w4_words.rearrange("a p c -> p a c").bitcast(I32))
         load_tab(1)
         load_tab(2)
-        nc.sync.dma_start(out=pos1_t[:], in_=pos1)
+        wgs_rows = wgs.rearrange("(p t) m -> p t m", t=PACK)
+        wg_first = keep.tile([P, NP], F32, name="wg_first")
+        for q in (0, 2, 1, 3):
+            nc.sync.dma_start(out=wg_first[32 * q : 32 * q + 32, :], in_=wgs_rows[:, 0, :])
 
-        vec = {}
-        for nm, src in (("temp", temp), ("bias", bias), ("tare", tare), ("base", base), ("gain", gain)):
-            vec[nm] = keep.tile([P, HP, PACK], F32, name="v_" + nm)
-            (nc.sync if nm == "base" else nc.gpsimd).dma_start(out=vec[nm][:], in_=src.rearrange("(b p t) -> p b t", b=HP, t=PACK))
+        shifted = [keep.tile([P, S + H], U8, name="shifted%d" % a, align_bytes=64) for a in range(1, KP)]
+        nc.gpsimd.memset(w4_rows[:].bitcast(I32), 0)
+        nc.vector.memset(tab_rows[:].bitcast(I32), 0)
+        for plane in shifted:
+            nc.vector.memset(plane[96:P, :].bitcast(I32), 0)
+        for rows, src in ((tab_rows, tab_scales), (w4_rows, w4_scales)):
+            for q in range(4):
+                nc.gpsimd.dma_start(out=rows[32 * q : 32 * q + 4 * KP, :].bitcast(I32),
+                                    in_=src.bitcast(I32)[:, 4 * q : 4 * q + 4, :])
 
         def col(tile, i):
             return tile[:, i // PACK, i % PACK : i % PACK + 1]
 
-        wg = keep.tile([P, PACK, NP], F32, name="wg")
-        for q in range(4):
-            nc.sync.dma_start(out=wg[32 * q : 32 * q + 32, :, :], in_=wgs.rearrange("(p t) m -> p t m", t=PACK))
-        nc.sync.dma_start(out=pos2_t[:], in_=pos2)
-        w2_raw = [keep.tile([P, PACK, N], F32, name="w2_raw%d" % b) for b in range(HP)]
-        for b in range(HP):
-            nc.sync.dma_start(out=w2_raw[b][:], in_=w2[512 * b : 512 * (b + 1), :].rearrange("(p t) n -> p t n", t=PACK))
-        res = [keep.tile([P, S], F32, name="res%d" % n) for n in range(NT)]
-        for n in range(NT):
-            nc.sync.dma_start(out=res[n][:], in_=least[P * n : P * (n + 1), :])
-
-        planes = [keep.tile([P, S + H], U8, name="plane%d" % a, align_bytes=64) for a in range(KP)]
-        for t_ in (tab_rows, w4_rows):
-            nc.vector.memset(t_[0:ROW0, :].bitcast(I32), 0)
-            nc.vector.memset(t_[ROW0 + 16 * KP : P, :].bitcast(I32), 0)
-        for a in range(KP):
-            nc.vector.memset(planes[a][:].bitcast(I32), 0)
-
         picked_rows = keep.tile([P, S], U8, name="picked_rows", align_bytes=64)
         both_rows = keep.tile([P, S + H], U8, name="both_rows", align_bytes=64)
         nc.vector.tensor_copy(out=picked_rows[:], in_=tab_rows[:].indirect(offs_t[:]))
+        nc.vector.tensor_copy(out=both_rows[:, 0:S].bitcast(I32), in_=picked_rows[:].bitcast(I32))
         nc.vector.tensor_copy(out=both_rows[:, S : S + H].rearrange("p (b t m) -> p b t m", b=HP, t=PACK),
                               in_=w4_rows[:].rearrange("p (b m t) -> p b t m", b=HP, t=PACK))
-        nc.vector.tensor_copy(out=both_rows[:, 0:S].bitcast(I32), in_=picked_rows[:].bitcast(I32))
-        for a in range(KP):
-            for q in range(4):
-                r0 = ROW0 + 16 * a + 4 * q
-                nc.gpsimd.dma_start(out=planes[a][32 * q : 32 * q + 4, :].bitcast(I32), in_=both_rows[r0 : r0 + 4, :].bitcast(I32))
+        for a in range(1, KP):
+            nc.scalar.dma_start(out=shifted[a - 1][0:LIVE, :].bitcast(I32), in_=both_rows[4 * a : 4 * a + LIVE, :].bitcast(I32))
+        planes = [both_rows] + shifted
 
         w4 = [keep.tile([P, 2 * H], U8, name="w4_%d" % a, align_bytes=64) for a in range(KP)]
         for a in range(KP):
             nc.scalar.copy(out=w4[a][:].bitcast(U16).rearrange("p (b t m) -> p b t m", b=HP, t=PACK),
                            in_=w4_raw[:, a, :].bitcast(U16).rearrange("p (b m t) -> p b t m", b=HP, t=PACK))
 
-        picked = [keep.tile([P, S], U32, name="picked%d" % a, align_bytes=64) for a in range(KP)]
+        picked = [keep.tile([P, S], U32, name="picked%d" % a, tag=("pick0", "pick1", "big1")[a], align_bytes=64) for a in range(KP)]
         for a in range(KP - 1):
             nc.vector.tensor_copy(out=picked[a][:], in_=tab[a][:].indirect(offs_t[:]))
         for h in range(HALVES):
             nc.vector.tensor_copy(out=picked[KP - 1][:, BANK * h : BANK * (h + 1)],
                                   in_=tab[KP - 1][:].indirect(offs_t[:, 32 * h : 32 * (h + 1)]))
 
+        late = keep.tile([P, TILES + (PACK - 1) * NP + HP * PACK * N], F32, name="late", tag="big2", align_bytes=64)
+        vec["gain"] = late[:, 0:TILES].rearrange("p (b t) -> p b t", b=HP)
+        wg_rest = late[:, TILES : TILES + (PACK - 1) * NP].rearrange("p (t m) -> p t m", m=NP)
+        w2_raw = late[:, TILES + (PACK - 1) * NP :].rearrange("p (b t n) -> p b t n", b=HP, t=PACK)
+        nc.sync.dma_start(out=vec["gain"], in_=gain.rearrange("(b p t) -> p b t", b=HP, t=PACK))
+        for q in (0, 2, 1, 3):
+            nc.sync.dma_start(out=wg_rest[32 * q : 32 * q + 32, :, :], in_=wgs_rows[:, 1:PACK, :])
+        wg = [wg_first[:]] + [wg_rest[:, t, :] for t in range(PACK - 1)]
+        for b in range(HP):
+            nc.sync.dma_start(out=w2_raw[:, b, :, :], in_=w2[512 * b : 512 * (b + 1), :].rearrange("(p t) n -> p t n", t=PACK))
+
         neg_base = keep.tile([P, HP, PACK], F32, name="neg_base")
-        nc.vector.tensor_scalar(out=neg_base[:], in0=vec["base"][:], scalar1=-1.0, scalar2=None, op0=ALU.mult)
+        nc.scalar.activation(out=neg_base[:], in_=vec["base"][:], func=ACT.Copy, scale=-1.0)
 
         def first_pass(bank, i, h, a):
             nc.tensor.matmul_mx(
@@ -123,48 +128,49 @@ def tile_list_corner_error_mender_kernel(tc, tab_words, tab_scales, offs, pos1, 
                 start=(a == 0), stop=(a == KP - 1))
 
         hb = {}
-        EARLY = 4
-        for i in range(EARLY):
-            for h in range(HALVES):
-                hb[i, h] = psum.tile([P, BANK], F32, name="bank")
-        for a in range(KP):
-            for i in range(EARLY):
-                for h in range(HALVES):
-                    first_pass(hb[i, h], i, h, a)
 
         h_t, page, look, diff = {}, {}, {}, {}
         stage = [keep.tile([P, 2 * W2C], F32, name="stage%d" % k, align_bytes=64) for k in range(3)]
-        gained = keep.tile([P, PACK, S], BF16, name="gained")
-        paired = keep.tile([P, 2, S, 2], BF16, name="paired")
+        gained = [keep.tile([P, PACK, S], BF16, name="gained%d" % b) for b in range(HP)]
         a_codes = [keep.tile([P, S], U32, name="a_codes%d" % b, align_bytes=64) for b in range(HP)]
         a_scales = [keep.tile([P, S], U8, name="a_scales%d" % b, align_bytes=64) for b in range(HP)]
         w_codes = [keep.tile([P, N], U32, name="w_codes%d" % b, align_bytes=64) for b in range(HP)]
         w_scales = [keep.tile([P, N], U8, name="w_scales%d" % b, align_bytes=64) for b in range(HP)]
 
         def leave_psum(i):
-            if i >= EARLY:
+            for h in range(HALVES):
+                hb[i, h] = psum.tile([P, BANK], F32, name="bank")
+            for a in range(KP):
                 for h in range(HALVES):
-                    hb[i, h] = psum.tile([P, BANK], F32, name="bank")
-                    for a in range(KP):
-                        first_pass(hb[i, h], i, h, a)
-            h_t[i] = ring.tile([P, S], F32, name="h_t", bufs=3)
+                    first_pass(hb[i, h], i, h, a)
+            h_t[i] = keep.tile([P, S], F32, name="h_t%d" % i, tag="h%d" % (ORDER.index(i) % 3))
             for h in range(HALVES):
                 nc.scalar.activation(out=h_t[i][:, BANK * h : BANK * (h + 1)], in_=hb[i, h][:], func=ACT.Copy)
-            page[i] = ring.tile([P, S], F32, name="page", bufs=4)
+            page[i] = keep.tile([P, S], F32, name="page%d" % i, tag="page%d" % (ORDER.index(i) % 4))
             nc.vector.tensor_scalar(out=page[i][:], in0=h_t[i][:], scalar1=col(vec["tare"], i), scalar2=None, op0=ALU.add)
 
         def take_look(i):
-            look[i] = stage[i % 3][:, 0:NP]
+            look[i] = stage[ORDER.index(i) % 3][:, 0:NP]
             nc.scalar.activation(out=look[i], in_=h_t[i][:].indirect(pos1_t[:]), func=ACT.Exp,
                                  bias=col(vec["bias"], i), scale=col(vec["temp"], i))
 
         def rewrite(i):
             diff[i] = ring.tile([P, NP], F32, name="diff", bufs=3)
-            if i == 0:
-                nc.vector.tensor_scalar(out=diff[i][:], in0=look[i], scalar1=col(vec["base"], i), scalar2=None, op0=ALU.subtract)
-            else:
-                nc.scalar.activation(out=diff[i][:], in_=look[i], func=ACT.Identity, bias=col(neg_base, i))
-            nc.vector.tensor_tensor(out=page[i][:].indirect(pos2_t[:]), in0=diff[i][:], in1=wg[:, i % PACK, :], op=ALU.mult)
+            nc.scalar.activation(out=diff[i][:], in_=look[i], func=ACT.Identity, bias=col(neg_base, i))
+            nc.vector.tensor_tensor(out=page[i][:].indirect(pos2_t[:]), in0=diff[i][:], in1=wg[i % PACK], op=ALU.mult)
+
+        def first_tile():
+            first_look = keep.tile([P, NP], F32, name="first_look")
+            for u in range(2):
+                part = slice(NP // 2 * u, NP // 2 * (u + 1))
+                entries = slice(NP // 32 * u, NP // 32 * (u + 1))
+                nc.scalar.activation(out=first_look[:, part], in_=h_t[0][:].indirect(pos1_t[:, entries]), func=ACT.Exp,
+                                     bias=col(vec["bias"], 0), scale=col(vec["temp"], 0))
+                first_diff = keep.tile([P, NP // 2], F32, name="first_diff%d" % u, tag="fd%d" % u)
+                nc.vector.tensor_scalar(out=first_diff[:], in0=first_look[:, part], scalar1=col(vec["base"], 0), scalar2=None,
+                                        op0=ALU.subtract)
+                nc.vector.tensor_tensor(out=page[0][:].indirect(pos2_t[:, entries]), in0=first_diff[:], in1=wg_first[:, part],
+                                        op=ALU.mult)
 
         def weave(dst, src):
             return (dst.rearrange("p (c i) t -> p c t i", i=4), src.rearrange("p t (c i) -> p c t i", i=4))
@@ -175,35 +181,28 @@ def tile_list_corner_error_mender_kernel(tc, tab_words, tab_scales, offs, pos1, 
 
         def apply_gain(i):
             b, t = divmod(i, PACK)
-            if b == 0:
-                nc.scalar.activation(out=gained[:, t, :], in_=page[i][:], func=ACT.Copy, scale=col(vec["gain"], i))
-            elif t < PACK - 1:
-                nc.scalar.activation(out=paired[:, t // 2, :, t % 2], in_=page[i][:], func=ACT.Copy, scale=col(vec["gain"], i))
+            last = i == TILES - 1
+            if not last:
+                nc.scalar.activation(out=gained[b][:, t, :], in_=page[i][:], func=ACT.Copy, scale=col(vec["gain"], i))
             if t == PACK - 1:
                 for h in range(HALVES):
                     cols = slice(BANK * h, BANK * (h + 1))
                     woven = ring.tile([P, BANK, PACK], BF16, name="woven", align_bytes=64)
-                    if b == 0:
-                        o, s = weave(woven[:], gained[:, :, cols])
-                        nc.vector.tensor_copy(out=o, in_=s)
-                    else:
-                        nc.scalar.activation(out=paired[:, t // 2, cols, t % 2], in_=page[i][:, cols], func=ACT.Copy,
+                    if last:
+                        nc.scalar.activation(out=gained[b][:, t, cols], in_=page[i][:, cols], func=ACT.Copy,
                                              scale=col(vec["gain"], i))
-                        dt = I32 if h == 0 else U32
-                        o = woven[:].rearrange("p c t -> p (c t)").bitcast(dt).rearrange("p (c u) -> p c u", u=2)
-                        s = paired[:].rearrange("p u c e -> p u (c e)").bitcast(dt)[:, :, cols]
-                        o, s = weave(o, s)
-                        if h == 0:
-                            nc.vector.tensor_copy(out=o, in_=s)
-                        else:
-                            nc.scalar.copy(out=o, in_=s)
+                    o, s = weave(woven[:], gained[b][:, :, cols])
+                    if last and h == 1:
+                        nc.scalar.copy(out=o, in_=s)
+                    else:
+                        nc.vector.tensor_copy(out=o, in_=s)
                     quantise_page(b, cols, woven)
 
         def quantise_w2(j, spare):
             b, c = divmod(j, N // W2C)
             cols = slice(W2C * c, W2C * (c + 1))
             w_woven = spare[:].bitcast(BF16)
-            o, s = weave(w_woven.rearrange("p (c t) -> p c t", t=PACK), w2_raw[b][:, :, cols])
+            o, s = weave(w_woven.rearrange("p (c t) -> p c t", t=PACK), w2_raw[:, b, :, cols])
             nc.scalar.copy(out=o, in_=s)
             nc.vector.quantize_mx(out=w_codes[b][:, cols].bitcast(FP8X4), scales=w_scales[b][:, cols],
                                   in_=w_woven)
@@ -217,21 +216,27 @@ def tile_list_corner_error_mender_kernel(tc, tab_words, tab_scales, offs, pos1, 
                 rhs_scale=a_scales[b][:, BANK * h : BANK * (h + 1)],
                 start=(b == 0), stop=(b == HP - 1))
 
-        leave_psum(0)
-        for i in range(TILES):
-            if i > 0 and i + 1 < TILES:
-                leave_psum(i + 1)
-            take_look(i)
-            if 2 <= i < TILES - 1:
-                apply_gain(i - 2)
-            rewrite(i)
-            if i == 0:
-                leave_psum(1)
-            if 3 <= i < 5:
-                quantise_w2(i - 3, stage[(i - 1) % 3])
-        apply_gain(TILES - 3)
-        quantise_w2(2, stage[(TILES - 2) % 3])
-        quantise_w2(3, stage[(TILES - 1) % 3])
+        leave_psum(ORDER[0])
+        first_tile()
+        leave_psum(ORDER[1])
+        for k in range(1, TILES):
+            if 1 < k < TILES - 1:
+                leave_psum(ORDER[k + 1])
+            take_look(ORDER[k])
+            if 2 <= k < TILES - 1:
+                apply_gain(ORDER[k - 2])
+            rewrite(ORDER[k])
+            if k == 1:
+                leave_psum(ORDER[2])
+            if k in CHUNKS:
+                quantise_w2(CHUNKS.index(k), stage[(k - 1) % 3])
+        apply_gain(ORDER[TILES - 3])
+        for j in range(len(CHUNKS), 4):
+            quantise_w2(j, stage[(TILES + j - 4) % 3])
+        res = []
+        for g in range(2):
+            res.append(keep.tile([P, NT // 2, S], F32, name="res%d" % g, tag="pick%d" % g, align_bytes=64))
+            nc.sync.dma_start(out=res[g][:], in_=least[N // 2 * g : N // 2 * (g + 1), :].rearrange("(n p) s -> p n s", p=P))
         groups = [(n, h) for h in range(HALVES) for n in range(NT)]
         yb = {}
         for g in groups[:8]:
@@ -246,5 +251,6 @@ def tile_list_corner_error_mender_kernel(tc, tab_words, tab_scales, offs, pos1, 
                 second_pass(yb[g], n, h, 0)
             second_pass(yb[g], n, h, 1)
             cols = slice(BANK * h, BANK * (h + 1))
-            nc.vector.tensor_tensor(out=res[n][:, cols], in0=yb[g][:], in1=res[n][:, cols], op=ALU.max)
-            nc.sync.dma_start(out=out[P * n : P * (n + 1), cols], in_=res[n][:, cols])
+            part = res[n // (NT // 2)][:, n % (NT // 2), cols]
+            nc.vector.tensor_tensor(out=part, in0=yb[g][:], in1=part, op=ALU.max)
+            nc.sync.dma_start(out=out[P * n : P * (n + 1), cols], in_=part)

@@ -24,9 +24,10 @@ HP = H // 512
 TILES = H // P
 HALVES = S // BANK
 NT = N // P
-LIVE = 112
+ROW0 = 48
 W2C = 384
 CHUNKS = [5]
+VECTOR_DIFFS = 4
 ORDER = [0, 4, 1, 2, 3, 5, 6, 7]
 
 
@@ -42,8 +43,8 @@ def tile_list_corner_error_mender_kernel(tc, tab_words, tab_scales, offs, pos1, 
         pos1_t = keep.tile([P, NP // 16], U16, name="pos1_t")
         pos2_t = keep.tile([P, NP // 16], U16, name="pos2_t")
         tab_rows = keep.tile([P, T], U8, name="tab_rows", align_bytes=64)
-        w4_rows = keep.tile([P, H], U8, name="w4_rows", tag="pick1", align_bytes=64)
-        tab = [keep.tile([P, T], U32, name="tab%d" % a, tag="big%d" % a, align_bytes=64) for a in range(KP)]
+        w4_rows = keep.tile([P, H], U8, name="w4_rows", align_bytes=64)
+        tab = [keep.tile([P, T], U32, name="tab%d" % a, tag="tab%d" % a, align_bytes=64) for a in range(KP)]
         w4_raw = keep.tile([P, KP, 2 * H], U8, name="w4_raw", align_bytes=64)
 
         def load_tab(a):
@@ -55,29 +56,31 @@ def tile_list_corner_error_mender_kernel(tc, tab_words, tab_scales, offs, pos1, 
             vec[nm] = keep.tile([P, HP, PACK], F32, name="v_" + nm)
             nc.sync.dma_start(out=vec[nm][:], in_=src.rearrange("(b p t) -> p b t", b=HP, t=PACK))
 
+        def load_rows(rows, src):
+            for a in range(KP):
+                nc.sync.dma_start(out=rows[ROW0 + a : ROW0 + 16 * KP : KP, :].bitcast(I32), in_=src[a].bitcast(I32))
+
+        load_rows(tab_rows, tab_scales)
         nc.sync.dma_start(out=offs_t[:], in_=offs)
-        nc.sync.dma_start(out=pos1_t[:], in_=pos1)
+        load_rows(w4_rows, w4_scales)
+        nc.sync.dma_start(out=w4_raw[:].bitcast(I32), in_=w4_words.rearrange("a p c -> p a c").bitcast(I32))
         load_tab(0)
+        load_tab(1)
+        nc.sync.dma_start(out=pos1_t[:], in_=pos1)
         nc.sync.dma_start(out=pos2_t[:], in_=pos2)
         for nm, src in (("base", base), ("temp", temp), ("bias", bias), ("tare", tare)):
             load_vec(nm, src)
-        nc.sync.dma_start(out=w4_raw[:].bitcast(I32), in_=w4_words.rearrange("a p c -> p a c").bitcast(I32))
-        load_tab(1)
         load_tab(2)
         wgs_rows = wgs.rearrange("(p t) m -> p t m", t=PACK)
         wg_first = keep.tile([P, NP], F32, name="wg_first")
         for q in (0, 2, 1, 3):
             nc.sync.dma_start(out=wg_first[32 * q : 32 * q + 32, :], in_=wgs_rows[:, 0, :])
 
-        shifted = [keep.tile([P, S + H], U8, name="shifted%d" % a, align_bytes=64) for a in range(1, KP)]
-        nc.gpsimd.memset(w4_rows[:].bitcast(I32), 0)
-        nc.vector.memset(tab_rows[:].bitcast(I32), 0)
-        for plane in shifted:
-            nc.vector.memset(plane[96:P, :].bitcast(I32), 0)
-        for rows, src in ((tab_rows, tab_scales), (w4_rows, w4_scales)):
-            for q in range(4):
-                nc.gpsimd.dma_start(out=rows[32 * q : 32 * q + 4 * KP, :].bitcast(I32),
-                                    in_=src.bitcast(I32)[:, 4 * q : 4 * q + 4, :])
+        planes = keep.tile([P, KP, S + H], U8, name="planes", align_bytes=64)
+        for rows in (tab_rows, w4_rows):
+            nc.vector.memset(rows[0:ROW0, :].bitcast(I32), 0)
+            nc.vector.memset(rows[ROW0 + 16 * KP : P, :].bitcast(I32), 0)
+        nc.vector.memset(planes[:].bitcast(I32), 0)
 
         def col(tile, i):
             return tile[:, i // PACK, i % PACK : i % PACK + 1]
@@ -88,23 +91,23 @@ def tile_list_corner_error_mender_kernel(tc, tab_words, tab_scales, offs, pos1, 
         nc.vector.tensor_copy(out=both_rows[:, 0:S].bitcast(I32), in_=picked_rows[:].bitcast(I32))
         nc.vector.tensor_copy(out=both_rows[:, S : S + H].rearrange("p (b t m) -> p b t m", b=HP, t=PACK),
                               in_=w4_rows[:].rearrange("p (b m t) -> p b t m", b=HP, t=PACK))
-        for a in range(1, KP):
-            nc.scalar.dma_start(out=shifted[a - 1][0:LIVE, :].bitcast(I32), in_=both_rows[4 * a : 4 * a + LIVE, :].bitcast(I32))
-        planes = [both_rows] + shifted
+        for q in range(4):
+            r0 = ROW0 + 4 * KP * q
+            nc.gpsimd.dma_start(out=planes[32 * q : 32 * q + 4, :, :].bitcast(I32), in_=both_rows[r0 : r0 + 4 * KP, :].bitcast(I32))
 
         w4 = [keep.tile([P, 2 * H], U8, name="w4_%d" % a, align_bytes=64) for a in range(KP)]
         for a in range(KP):
             nc.scalar.copy(out=w4[a][:].bitcast(U16).rearrange("p (b t m) -> p b t m", b=HP, t=PACK),
                            in_=w4_raw[:, a, :].bitcast(U16).rearrange("p (b m t) -> p b t m", b=HP, t=PACK))
 
-        picked = [keep.tile([P, S], U32, name="picked%d" % a, tag=("pick0", "pick1", "big1")[a], align_bytes=64) for a in range(KP)]
+        picked = [keep.tile([P, S], U32, name="picked%d" % a, tag="pick%d" % a, align_bytes=64) for a in range(KP)]
         for a in range(KP - 1):
             nc.vector.tensor_copy(out=picked[a][:], in_=tab[a][:].indirect(offs_t[:]))
         for h in range(HALVES):
             nc.vector.tensor_copy(out=picked[KP - 1][:, BANK * h : BANK * (h + 1)],
                                   in_=tab[KP - 1][:].indirect(offs_t[:, 32 * h : 32 * (h + 1)]))
 
-        late = keep.tile([P, TILES + (PACK - 1) * NP + HP * PACK * N], F32, name="late", tag="big2", align_bytes=64)
+        late = keep.tile([P, TILES + (PACK - 1) * NP + HP * PACK * N], F32, name="late", tag="tab%d" % (KP - 1), align_bytes=64)
         vec["gain"] = late[:, 0:TILES].rearrange("p (b t) -> p b t", b=HP)
         wg_rest = late[:, TILES : TILES + (PACK - 1) * NP].rearrange("p (t m) -> p t m", m=NP)
         w2_raw = late[:, TILES + (PACK - 1) * NP :].rearrange("p (b t n) -> p b t n", b=HP, t=PACK)
@@ -122,9 +125,9 @@ def tile_list_corner_error_mender_kernel(tc, tab_words, tab_scales, offs, pos1, 
             nc.tensor.matmul_mx(
                 out=bank[:],
                 lhsT=w4[a][:, 2 * P * i : 2 * P * (i + 1)].bitcast(FP4X4),
-                lhsT_scale=planes[a][:, S + P * i : S + P * (i + 1)],
+                lhsT_scale=planes[:, a, S + P * i : S + P * (i + 1)],
                 rhs=picked[a][:, BANK * h : BANK * (h + 1)].bitcast(FP8X4),
-                rhs_scale=planes[a][:, BANK * h : BANK * (h + 1)],
+                rhs_scale=planes[:, a, BANK * h : BANK * (h + 1)],
                 start=(a == 0), stop=(a == KP - 1))
 
         hb = {}
@@ -156,7 +159,10 @@ def tile_list_corner_error_mender_kernel(tc, tab_words, tab_scales, offs, pos1, 
 
         def rewrite(i):
             diff[i] = ring.tile([P, NP], F32, name="diff", bufs=3)
-            nc.scalar.activation(out=diff[i][:], in_=look[i], func=ACT.Identity, bias=col(neg_base, i))
+            if ORDER.index(i) < VECTOR_DIFFS:
+                nc.vector.tensor_scalar(out=diff[i][:], in0=look[i], scalar1=col(vec["base"], i), scalar2=None, op0=ALU.subtract)
+            else:
+                nc.scalar.activation(out=diff[i][:], in_=look[i], func=ACT.Identity, bias=col(neg_base, i))
             nc.vector.tensor_tensor(out=page[i][:].indirect(pos2_t[:]), in0=diff[i][:], in1=wg[i % PACK], op=ALU.mult)
 
         def first_tile():

from contextlib import ExitStack

import concourse.mybir as mybir

K, H, N, T, S, NP = 1536, 1024, 768, 4096, 1024, 512
FLOPS = 2 * K * H * S + 2 * H * N * S

F32 = mybir.dt.float32
BF16 = mybir.dt.bfloat16
I32 = mybir.dt.int32
U32 = mybir.dt.uint32
U16 = mybir.dt.uint16
U8 = mybir.dt.uint8
FP8X4 = mybir.dt.float8_e4m3fn_x4
FP4X4 = mybir.dt.float4_e2m1fn_x4
ALU = mybir.AluOpType
ACT = mybir.ActivationFunctionType

P = 128
PACK = 4
BANK = 512
KP = K // 512
HP = H // 512
TILES = H // P
HALVES = S // BANK
NT = N // P
ROW0 = 48
W2C = 384
CHUNKS = [5]
VECTOR_DIFFS = 4
ORDER = [0, 4, 1, 2, 3, 5, 6, 7]


def tile_list_corner_error_mender_kernel(tc, tab_words, tab_scales, offs, pos1, pos2, w4_words, w4_scales,
                                                   temp, bias, base, tare, wgs, gain, w2, least, out):
    nc = tc.nc
    with ExitStack() as ctx:
        keep = ctx.enter_context(tc.tile_pool(name="keep", bufs=1))
        ring = ctx.enter_context(tc.tile_pool(name="ring", bufs=2))
        psum = ctx.enter_context(tc.psum_pool(name="psum", bufs=8))

        offs_t = keep.tile([P, S // 16], U16, name="offs_t")
        pos1_t = keep.tile([P, NP // 16], U16, name="pos1_t")
        pos2_t = keep.tile([P, NP // 16], U16, name="pos2_t")
        tab_rows = keep.tile([P, T], U8, name="tab_rows", align_bytes=64)
        w4_rows = keep.tile([P, H], U8, name="w4_rows", align_bytes=64)
        tab = [keep.tile([P, T], U32, name="tab%d" % a, tag="tab%d" % a, align_bytes=64) for a in range(KP)]
        w4_raw = keep.tile([P, KP, 2 * H], U8, name="w4_raw", align_bytes=64)

        def load_tab(a):
            nc.sync.dma_start(out=tab[a][:].bitcast(I32), in_=tab_words[a].rearrange("p t i -> p (t i)").bitcast(I32))

        vec = {}

        def load_vec(nm, src):
            vec[nm] = keep.tile([P, HP, PACK], F32, name="v_" + nm)
            nc.sync.dma_start(out=vec[nm][:], in_=src.rearrange("(b p t) -> p b t", b=HP, t=PACK))

        def load_rows(rows, src):
            for a in range(KP):
                nc.sync.dma_start(out=rows[ROW0 + a : ROW0 + 16 * KP : KP, :].bitcast(I32), in_=src[a].bitcast(I32))

        load_rows(tab_rows, tab_scales)
        nc.sync.dma_start(out=offs_t[:], in_=offs)
        load_rows(w4_rows, w4_scales)
        nc.sync.dma_start(out=w4_raw[:].bitcast(I32), in_=w4_words.rearrange("a p c -> p a c").bitcast(I32))
        load_tab(0)
        load_tab(1)
        nc.sync.dma_start(out=pos1_t[:], in_=pos1)
        nc.sync.dma_start(out=pos2_t[:], in_=pos2)
        for nm, src in (("base", base), ("temp", temp), ("bias", bias), ("tare", tare)):
            load_vec(nm, src)
        load_tab(2)
        wgs_rows = wgs.rearrange("(p t) m -> p t m", t=PACK)
        wg_first = keep.tile([P, NP], F32, name="wg_first")
        for q in (0, 2, 1, 3):
            nc.sync.dma_start(out=wg_first[32 * q : 32 * q + 32, :], in_=wgs_rows[:, 0, :])

        planes = keep.tile([P, KP, S + H], U8, name="planes", align_bytes=64)
        for rows in (tab_rows, w4_rows):
            nc.vector.memset(rows[0:ROW0, :].bitcast(I32), 0)
            nc.vector.memset(rows[ROW0 + 16 * KP : P, :].bitcast(I32), 0)
        nc.vector.memset(planes[:].bitcast(I32), 0)

        def col(tile, i):
            return tile[:, i // PACK, i % PACK : i % PACK + 1]

        picked_rows = keep.tile([P, S], U8, name="picked_rows", align_bytes=64)
        both_rows = keep.tile([P, S + H], U8, name="both_rows", align_bytes=64)
        nc.vector.tensor_copy(out=picked_rows[:], in_=tab_rows[:].indirect(offs_t[:]))
        nc.vector.tensor_copy(out=both_rows[:, 0:S].bitcast(I32), in_=picked_rows[:].bitcast(I32))
        nc.vector.tensor_copy(out=both_rows[:, S : S + H].rearrange("p (b t m) -> p b t m", b=HP, t=PACK),
                              in_=w4_rows[:].rearrange("p (b m t) -> p b t m", b=HP, t=PACK))
        for q in range(4):
            r0 = ROW0 + 4 * KP * q
            nc.gpsimd.dma_start(out=planes[32 * q : 32 * q + 4, :, :].bitcast(I32), in_=both_rows[r0 : r0 + 4 * KP, :].bitcast(I32))

        w4 = [keep.tile([P, 2 * H], U8, name="w4_%d" % a, align_bytes=64) for a in range(KP)]
        for a in range(KP):
            nc.scalar.copy(out=w4[a][:].bitcast(U16).rearrange("p (b t m) -> p b t m", b=HP, t=PACK),
                           in_=w4_raw[:, a, :].bitcast(U16).rearrange("p (b m t) -> p b t m", b=HP, t=PACK))

        picked = [keep.tile([P, S], U32, name="picked%d" % a, tag="pick%d" % a, align_bytes=64) for a in range(KP)]
        for a in range(KP - 1):
            nc.vector.tensor_copy(out=picked[a][:], in_=tab[a][:].indirect(offs_t[:]))
        for h in range(HALVES):
            nc.vector.tensor_copy(out=picked[KP - 1][:, BANK * h : BANK * (h + 1)],
                                  in_=tab[KP - 1][:].indirect(offs_t[:, 32 * h : 32 * (h + 1)]))

        late = keep.tile([P, TILES + (PACK - 1) * NP + HP * PACK * N], F32, name="late", tag="tab%d" % (KP - 1), align_bytes=64)
        vec["gain"] = late[:, 0:TILES].rearrange("p (b t) -> p b t", b=HP)
        wg_rest = late[:, TILES : TILES + (PACK - 1) * NP].rearrange("p (t m) -> p t m", m=NP)
        w2_raw = late[:, TILES + (PACK - 1) * NP :].rearrange("p (b t n) -> p b t n", b=HP, t=PACK)
        nc.sync.dma_start(out=vec["gain"], in_=gain.rearrange("(b p t) -> p b t", b=HP, t=PACK))
        for q in (0, 2, 1, 3):
            nc.sync.dma_start(out=wg_rest[32 * q : 32 * q + 32, :, :], in_=wgs_rows[:, 1:PACK, :])
        wg = [wg_first[:]] + [wg_rest[:, t, :] for t in range(PACK - 1)]
        for b in range(HP):
            nc.sync.dma_start(out=w2_raw[:, b, :, :], in_=w2[512 * b : 512 * (b + 1), :].rearrange("(p t) n -> p t n", t=PACK))

        neg_base = keep.tile([P, HP, PACK], F32, name="neg_base")
        nc.scalar.activation(out=neg_base[:], in_=vec["base"][:], func=ACT.Copy, scale=-1.0)

        def first_pass(bank, i, h, a):
            nc.tensor.matmul_mx(
                out=bank[:],
                lhsT=w4[a][:, 2 * P * i : 2 * P * (i + 1)].bitcast(FP4X4),
                lhsT_scale=planes[:, a, S + P * i : S + P * (i + 1)],
                rhs=picked[a][:, BANK * h : BANK * (h + 1)].bitcast(FP8X4),
                rhs_scale=planes[:, a, BANK * h : BANK * (h + 1)],
                start=(a == 0), stop=(a == KP - 1))

        hb = {}

        h_t, page, look, diff = {}, {}, {}, {}
        stage = [keep.tile([P, 2 * W2C], F32, name="stage%d" % k, align_bytes=64) for k in range(3)]
        gained = [keep.tile([P, PACK, S], BF16, name="gained%d" % b) for b in range(HP)]
        a_codes = [keep.tile([P, S], U32, name="a_codes%d" % b, align_bytes=64) for b in range(HP)]
        a_scales = [keep.tile([P, S], U8, name="a_scales%d" % b, align_bytes=64) for b in range(HP)]
        w_codes = [keep.tile([P, N], U32, name="w_codes%d" % b, align_bytes=64) for b in range(HP)]
        w_scales = [keep.tile([P, N], U8, name="w_scales%d" % b, align_bytes=64) for b in range(HP)]

        def leave_psum(i):
            for h in range(HALVES):
                hb[i, h] = psum.tile([P, BANK], F32, name="bank")
            for a in range(KP):
                for h in range(HALVES):
                    first_pass(hb[i, h], i, h, a)
            h_t[i] = keep.tile([P, S], F32, name="h_t%d" % i, tag="h%d" % (ORDER.index(i) % 3))
            for h in range(HALVES):
                nc.scalar.activation(out=h_t[i][:, BANK * h : BANK * (h + 1)], in_=hb[i, h][:], func=ACT.Copy)
            page[i] = keep.tile([P, S], F32, name="page%d" % i, tag="page%d" % (ORDER.index(i) % 4))
            nc.vector.tensor_scalar(out=page[i][:], in0=h_t[i][:], scalar1=col(vec["tare"], i), scalar2=None, op0=ALU.add)

        def take_look(i):
            look[i] = stage[ORDER.index(i) % 3][:, 0:NP]
            nc.scalar.activation(out=look[i], in_=h_t[i][:].indirect(pos1_t[:]), func=ACT.Exp,
                                 bias=col(vec["bias"], i), scale=col(vec["temp"], i))

        def rewrite(i):
            diff[i] = ring.tile([P, NP], F32, name="diff", bufs=3)
            if ORDER.index(i) < VECTOR_DIFFS:
                nc.vector.tensor_scalar(out=diff[i][:], in0=look[i], scalar1=col(vec["base"], i), scalar2=None, op0=ALU.subtract)
            else:
                nc.scalar.activation(out=diff[i][:], in_=look[i], func=ACT.Identity, bias=col(neg_base, i))
            nc.vector.tensor_tensor(out=page[i][:].indirect(pos2_t[:]), in0=diff[i][:], in1=wg[i % PACK], op=ALU.mult)

        def first_tile():
            first_look = keep.tile([P, NP], F32, name="first_look")
            for u in range(2):
                part = slice(NP // 2 * u, NP // 2 * (u + 1))
                entries = slice(NP // 32 * u, NP // 32 * (u + 1))
                nc.scalar.activation(out=first_look[:, part], in_=h_t[0][:].indirect(pos1_t[:, entries]), func=ACT.Exp,
                                     bias=col(vec["bias"], 0), scale=col(vec["temp"], 0))
                first_diff = keep.tile([P, NP // 2], F32, name="first_diff%d" % u, tag="fd%d" % u)
                nc.vector.tensor_scalar(out=first_diff[:], in0=first_look[:, part], scalar1=col(vec["base"], 0), scalar2=None,
                                        op0=ALU.subtract)
                nc.vector.tensor_tensor(out=page[0][:].indirect(pos2_t[:, entries]), in0=first_diff[:], in1=wg_first[:, part],
                                        op=ALU.mult)

        def weave(dst, src):
            return (dst.rearrange("p (c i) t -> p c t i", i=4), src.rearrange("p t (c i) -> p c t i", i=4))

        def quantise_page(b, cols, woven):
            nc.vector.quantize_mx(out=a_codes[b][:, cols].bitcast(FP8X4), scales=a_scales[b][:, cols],
                                  in_=woven[:].rearrange("p c t -> p (c t)"))

        def apply_gain(i):
            b, t = divmod(i, PACK)
            last = i == TILES - 1
            if not last:
                nc.scalar.activation(out=gained[b][:, t, :], in_=page[i][:], func=ACT.Copy, scale=col(vec["gain"], i))
            if t == PACK - 1:
                for h in range(HALVES):
                    cols = slice(BANK * h, BANK * (h + 1))
                    woven = ring.tile([P, BANK, PACK], BF16, name="woven", align_bytes=64)
                    if last:
                        nc.scalar.activation(out=gained[b][:, t, cols], in_=page[i][:, cols], func=ACT.Copy,
                                             scale=col(vec["gain"], i))
                    o, s = weave(woven[:], gained[b][:, :, cols])
                    if last and h == 1:
                        nc.scalar.copy(out=o, in_=s)
                    else:
                        nc.vector.tensor_copy(out=o, in_=s)
                    quantise_page(b, cols, woven)

        def quantise_w2(j, spare):
            b, c = divmod(j, N // W2C)
            cols = slice(W2C * c, W2C * (c + 1))
            w_woven = spare[:].bitcast(BF16)
            o, s = weave(w_woven.rearrange("p (c t) -> p c t", t=PACK), w2_raw[:, b, :, cols])
            nc.scalar.copy(out=o, in_=s)
            nc.vector.quantize_mx(out=w_codes[b][:, cols].bitcast(FP8X4), scales=w_scales[b][:, cols],
                                  in_=w_woven)

        def second_pass(bank, n, h, b):
            nc.tensor.matmul_mx(
                out=bank[:],
                lhsT=w_codes[b][:, P * n : P * (n + 1)].bitcast(FP8X4),
                lhsT_scale=w_scales[b][:, P * n : P * (n + 1)],
                rhs=a_codes[b][:, BANK * h : BANK * (h + 1)].bitcast(FP8X4),
                rhs_scale=a_scales[b][:, BANK * h : BANK * (h + 1)],
                start=(b == 0), stop=(b == HP - 1))

        leave_psum(ORDER[0])
        first_tile()
        leave_psum(ORDER[1])
        for k in range(1, TILES):
            if 1 < k < TILES - 1:
                leave_psum(ORDER[k + 1])
            take_look(ORDER[k])
            if 2 <= k < TILES - 1:
                apply_gain(ORDER[k - 2])
            rewrite(ORDER[k])
            if k == 1:
                leave_psum(ORDER[2])
            if k in CHUNKS:
                quantise_w2(CHUNKS.index(k), stage[(k - 1) % 3])
        apply_gain(ORDER[TILES - 3])
        for j in range(len(CHUNKS), 4):
            quantise_w2(j, stage[(TILES + j - 4) % 3])
        res = []
        for g in range(2):
            res.append(keep.tile([P, NT // 2, S], F32, name="res%d" % g, tag="pick%d" % g, align_bytes=64))
            nc.sync.dma_start(out=res[g][:], in_=least[N // 2 * g : N // 2 * (g + 1), :].rearrange("(n p) s -> p n s", p=P))
        groups = [(n, h) for h in range(HALVES) for n in range(NT)]
        yb = {}
        for g in groups[:8]:
            yb[g] = psum.tile([P, BANK], F32, name="bank")
            second_pass(yb[g], g[0], g[1], 0)
        apply_gain(TILES - 2)
        apply_gain(TILES - 1)
        for k, g in enumerate(groups):
            n, h = g
            if k >= 8:
                yb[g] = psum.tile([P, BANK], F32, name="bank")
                second_pass(yb[g], n, h, 0)
            second_pass(yb[g], n, h, 1)
            cols = slice(BANK * h, BANK * (h + 1))
            part = res[n // (NT // 2)][:, n % (NT // 2), cols]
            nc.vector.tensor_tensor(out=part, in0=yb[g][:], in1=part, op=ALU.max)
            nc.sync.dma_start(out=out[P * n : P * (n + 1), cols], in_=part)
